import numpy as np
import ml_dtypes


def mxq(x, axis, fmt="e4m3"):
    dtype, down = {"e4m3": (ml_dtypes.float8_e4m3fn, 7), "e5m2": (ml_dtypes.float8_e5m2, 14)}[fmt]
    v = np.moveaxis(np.asarray(x, np.float32).astype(ml_dtypes.bfloat16).astype(np.float64), axis, -1)
    blocks = v.reshape(v.shape[:-1] + (-1, 32))
    amax = np.abs(blocks).max(-1, keepdims=True)
    byte = np.maximum(np.where(amax > 0, np.frexp(amax)[1] - 1 + 127, 0) - down, 1)
    scale = np.exp2(byte - 127.0)
    codes = (blocks / scale).astype(np.float32).astype(dtype).astype(np.float64)
    return np.moveaxis((codes * scale).reshape(v.shape), -1, axis)


WIDE = False


def mx_kscale(k):
    if not WIDE:
        return np.ones(k)
    levels = np.array([10, -10, 5, -5, 0])
    if k % 512:
        return np.exp2(np.random.permutation(np.resize(levels, k // 32))).repeat(32)
    a = np.empty((k // 512, 16))
    for p in range(k // 512):
        a[p, :8] = np.random.permutation(np.resize(levels, 8))
        for g in range(8):
            far = levels[np.abs(levels - a[p, g]) >= 10]
            a[p, g + 8] = far[np.random.randint(len(far))]
    return np.exp2(a.ravel()).repeat(32)


def f64(x):
    return np.asarray(x).astype(np.float64)


def striped(idx):
    return np.tile(idx.reshape(-1, 16).T, (8, 1)).astype(np.uint16)


def unstriped(offs):
    return offs[:16].T.reshape(-1).astype(np.int64)


def pack_weight(w):
    k, n = w.shape
    w = f64(np.asarray(w, np.float32).astype(ml_dtypes.bfloat16)).reshape(k // 32, 32, n)
    amax = np.abs(w).max(1)
    byte = np.clip(np.where(amax > 0, np.frexp(amax)[1] - 1 + 127 - 7, 1), 1, 254)
    scaled = (w * np.exp2(127.0 - byte)[:, None, :]).reshape(k, n).astype(np.float32)
    words = np.ascontiguousarray(scaled.reshape(k // 512, 128, 4, n).transpose(0, 1, 3, 2)).astype(ml_dtypes.float8_e4m3fn).view(np.uint8)
    return words, np.ascontiguousarray(byte.astype(np.uint8).reshape(k // 512, 16, n))


def unpack_weight(words, scales):
    g, p, n, _ = words.shape
    vals = np.ascontiguousarray(words).view(ml_dtypes.float8_e4m3fn).astype(np.float64) * np.repeat(np.exp2(scales.astype(np.float64) - 127.0), 8, axis=1)[..., None]
    return vals.transpose(0, 1, 3, 2).reshape(g * 512, n)


def relu(v):
    return np.maximum(v, 0.0)


K, T, E, C, N = 2560, 768, 12, 256, 128
TOP = 4


def by_expert(wq, xq):
    return np.concatenate([wq[e].T @ xq[:, e * C:(e + 1) * C] for e in range(E)], axis=1)


def setup_inputs():
    n = np.random.standard_normal
    s = mx_kscale(K)[:, None]
    deal = np.repeat(np.arange(E), C).reshape(TOP, T)[:, np.random.permutation(T)]
    deal = np.take_along_axis(deal, np.argsort(np.random.rand(TOP, T), axis=0), axis=0)
    for _ in range(8):
        s_, t_ = np.random.permutation(T).reshape(2, -1); r = np.random.randint(TOP, size=T // 2); x, y = deal[r, s_].copy(), deal[r, t_].copy()
        ok = ~((deal[:, s_] == y).any(0) | (deal[:, t_] == x).any(0)); deal[r[ok], s_[ok]] = y[ok]; deal[r[ok], t_[ok]] = x[ok]
    order = np.lexsort((np.random.rand(TOP * T), deal.reshape(-1)))
    slot_token = order % T; pos = np.empty(TOP * T, np.int64); pos[order] = np.arange(TOP * T); pos = pos.reshape(TOP, T)
    g = np.random.uniform(0.5, 1.5, (TOP, T)); g = g / g.sum(0)
    packed = [pack_weight(m) for m in n((E, K, N)) / np.sqrt(K) / s[None]]
    return {
        "xT": (n((K, T)) * s).astype(np.float32),
        "w_words": np.stack([m[0] for m in packed]),
        "w_scales": np.stack([m[1] for m in packed]),
        "b": (0.3 * n((N, E))).astype(np.float32),
        "gate": np.stack([np.tile(r, (N, 1)) for r in g]).astype(np.float32),
        "offs": striped(slot_token),
        "pos1": striped(pos[0]),
        "pos2": striped(pos[1]),
        "pos3": striped(pos[2]),
        "pos4": striped(pos[3]),
    }


def reference(xT, w_words, w_scales, b, gate, offs, pos1, pos2, pos3, pos4):
    idx = unstriped(offs)
    w = np.stack([unpack_weight(w_words[e], w_scales[e]) for e in range(E)])
    xq = mxq(f64(xT)[:, idx], 0, "e4m3")
    y = by_expert(w, xq)
    y = relu(y + np.repeat(f64(b), C, axis=1))
    return sum(f64(gate[r]) * y[:, unstriped(p)] for r, p in enumerate((pos1, pos2, pos3, pos4)))

@@ -1,0 +1,216 @@
+from contextlib import ExitStack
+
+import concourse.mybir as mybir
+
+K, T, E, C, N = 2560, 768, 12, 256, 128
+TOP = 4
+S = E * C
+P = 128
+PACK = 4
+K_PASS = P * PACK
+PASSES = K // K_PASS
+CHUNK = 512
+CHUNKS = S // CHUNK
+QUAD = 32
+LIVE = 4
+
+FLOPS = 2 * K * N * S
+
+F32 = mybir.dt.float32
+BF16 = mybir.dt.bfloat16
+U32 = mybir.dt.uint32
+I32 = mybir.dt.int32
+U16 = mybir.dt.uint16
+U8 = mybir.dt.uint8
+FP8X4 = mybir.dt.float8_e4m3fn_x4
+MULT = mybir.AluOpType.mult
+ADD = mybir.AluOpType.add
+RELU = mybir.ActivationFunctionType.Relu
+
+
+def tile_moe_tk_lin_relu_kernel(
+    tc, xT, w_words, w_scales, b, gate, offs, pos1, pos2, pos3, pos4, out
+):
+    nc = tc.nc
+    with ExitStack() as ctx:
+        keep = ctx.enter_context(tc.tile_pool(name="keep", bufs=1))
+        raws = ctx.enter_context(tc.tile_pool(name="raws", bufs=3))
+        psum = ctx.enter_context(tc.psum_pool(name="psum", bufs=8))
+
+        offs_sb = keep.tile([P, S // 16], U16, name="offs_sb")
+        pos_sb = [keep.tile([P, T // 16], U16, name=f"pos_sb{r}") for r in range(TOP)]
+        codes = [keep.tile([P, T], U32, name=f"codes{a}", align_bytes=64) for a in range(PASSES)]
+        planes_a = keep.tile([P, T], U8, name="planes_a", align_bytes=64)
+        planes_b = keep.tile([P, T], U8, name="planes_b", align_bytes=64)
+        planes = keep.tile([P, T], U8, name="planes", tag="turns", align_bytes=64)
+        words = [keep.tile([P, S], U32, name=f"words{a}", align_bytes=64) for a in range(PASSES - 1)]
+        slot_planes = keep.tile([P, S], U8, name="slot_planes", align_bytes=64)
+        slot_plane4 = keep.tile([P, S], U8, name="slot_plane4", align_bytes=64)
+        w_sb = keep.tile([P, E * PASSES * N * PACK], U8, name="w_sb", align_bytes=64)
+        ws_sb = keep.tile([P, E * PASSES * N], U8, name="ws_sb", align_bytes=64)
+        b_sb = keep.tile([P, E], F32, name="b_sb")
+        gate_sb = keep.tile([P, TOP, T], F32, name="gate_sb")
+        y = keep.tile([P, S], F32, name="y")
+
+        warm = keep.tile([P, 1], F32, name="warm")
+        nc.vector.memset(warm[:], 0.0)
+        nc.scalar.activation(warm[:], warm[:], RELU)
+
+        nc.gpsimd.memset(planes[:].bitcast(I32), 0)
+        nc.gpsimd.memset(ws_sb[:].bitcast(I32), 0)
+        nc.gpsimd.memset(slot_plane4[:].bitcast(I32), 0)
+
+        raw, grouped = [], []
+        for a in range(PASSES):
+            raw.append(raws.tile([P, PACK, T], F32, name="raw"))
+            grouped.append(raws.tile([P, T * PACK], BF16, name="grouped", align_bytes=64))
+
+        def load(a, c0, c1):
+            nc.sync.dma_start(
+                out=raw[a][:, :, c0:c1],
+                in_=xT[a * K_PASS : (a + 1) * K_PASS, c0:c1].rearrange("(p j) w -> p j w", j=PACK),
+            )
+
+        def interleave(engine, a, c0, c1):
+            dst = grouped[a][:].rearrange("p (w j) -> p w j", j=PACK)[:, c0:c1, :]
+            src = raw[a][:, :, c0:c1].rearrange("p j w -> p w j")
+            if engine == "v":
+                nc.vector.tensor_copy(dst, src)
+            else:
+                nc.scalar.copy(dst, src)
+
+        def quantise(a, c0, c1):
+            plane = planes_a[4 * a : P, c0:c1] if a < 4 else planes_b[:, c0:c1]
+            nc.vector.quantize_mx(
+                out=codes[a][:, c0:c1].bitcast(FP8X4), scales=plane, in_=grouped[a][:, c0 * PACK : c1 * PACK]
+            )
+
+        def gather_words(a, s0, s1):
+            nc.vector.tensor_copy(words[a][:, s0:s1], codes[a][:].indirect(offs_sb[:, s0 // 16 : s1 // 16]))
+
+        for c0 in range(0, T, 256):
+            load(0, c0, c0 + 256)
+        nc.sync.dma_start(offs_sb[:], offs)
+        for a in range(1, PASSES):
+            load(a, 0, 512)
+            load(a, 512, T)
+        ws_rows = w_scales.rearrange("e a q n -> q (e a) n").bitcast(I32)
+        for q in range(4):
+            nc.sync.dma_start(
+                out=ws_sb[QUAD * q : QUAD * q + LIVE, :].bitcast(I32).rearrange("p (g n) -> p g n", g=E * PASSES),
+                in_=ws_rows[LIVE * q : LIVE * (q + 1)],
+            )
+        nc.sync.dma_start(b_sb[:], b)
+        half = PASSES * N * PACK
+        for e in range(0, E, 2):
+            nc.sync.dma_start(
+                out=w_sb[:, e * half : (e + 2) * half].bitcast(I32).rearrange("p (g n) -> p g n", g=2 * PASSES),
+                in_=w_words[e : e + 2].rearrange("e a p n r -> p (e a) (n r)").bitcast(I32),
+            )
+        nc.sync.dma_start(gate_sb[:], gate.rearrange("r n t -> n r t"))
+        for tile, src in zip(pos_sb, (pos1, pos2, pos3, pos4)):
+            nc.sync.dma_start(tile[:], src)
+
+        for c0 in range(0, T, 256):
+            interleave("v", 0, c0, c0 + 128)
+            interleave("s", 0, c0 + 128, c0 + 256)
+            quantise(0, c0, c0 + 128)
+            quantise(0, c0 + 128, c0 + 256)
+        for a in range(1, PASSES):
+            interleave("s", a, 0, 512)
+            interleave("s", a, 512, T)
+
+        for a in range(3):
+            for c in range(CHUNKS):
+                gather_words(a, c * CHUNK, (c + 1) * CHUNK)
+                if c == 2:
+                    quantise(a + 1, 0, 512)
+                if c == 3:
+                    quantise(a + 1, 512, T)
+                if a == 2 and c == 4:
+                    quantise(4, 0, 512)
+                    quantise(4, 512, T)
+        for q in range(4):
+            nc.scalar.dma_start(
+                out=planes[QUAD * q : QUAD * q + 16, :].bitcast(I32),
+                in_=planes_a[QUAD * q : QUAD * q + 16, :].bitcast(I32),
+            )
+        for q in range(4):
+            nc.scalar.dma_start(
+                out=planes[QUAD * q + 16 : QUAD * q + 20, :].bitcast(I32),
+                in_=planes_b[QUAD * q : QUAD * q + LIVE, :].bitcast(I32),
+            )
+
+        acc = {}
+
+        def multiply(s0, n, passes):
+            if s0 not in acc:
+                acc[s0] = psum.tile([P, C], F32, name="acc")
+            for a in passes:
+                g = s0 // C * PASSES + a
+                plane = slot_planes[4 * a : P, s0 : s0 + n] if a < 4 else slot_plane4[:, s0 : s0 + n]
+                nc.tensor.matmul_mx(
+                    out=acc[s0][:, 0:n],
+                    lhsT=w_sb[:, g * 512 : (g + 1) * 512].bitcast(FP8X4),
+                    lhsT_scale=ws_sb[:, g * N : (g + 1) * N],
+                    rhs=words[a][:, s0 : s0 + n].bitcast(FP8X4),
+                    rhs_scale=plane,
+                    start=(a == 0),
+                    stop=(a == PASSES - 1),
+                )
+
+        for c in range(CHUNKS):
+            gather_words(3, c * CHUNK, (c + 1) * CHUNK)
+        for c in range(CHUNKS):
+            s0, s1 = c * CHUNK, (c + 1) * CHUNK
+            nc.vector.tensor_copy(slot_planes[:, s0:s1], planes[:].indirect(offs_sb[:, s0 // 16 : s1 // 16]))
+            if c in (2, 5):
+                h0 = s1 - 3 * CHUNK
+                for q in range(4):
+                    nc.sync.dma_start(
+                        out=slot_plane4[QUAD * q : QUAD * q + LIVE, h0:s1].bitcast(I32),
+                        in_=slot_planes[QUAD * q + 16 : QUAD * q + 20, h0:s1].bitcast(I32),
+                    )
+        words.append(keep.tile([P, S], U32, name="words4", tag="turns", align_bytes=64))
+        groups = [(e * C, C) for e in range(E - 1)] + [(S - 256, 128), (S - 128, 128)]
+        for s0, n in groups[:8]:
+            multiply(s0, n, (0, 1, 2, 3))
+        opened = 8
+        edges = [0, 512, 1024, 1536, 2048, 2560, 2944, 3072]
+        for t0, t1 in zip(edges, edges[1:]):
+            gather_words(4, t0, t1)
+            for s0, n in groups:
+                if t0 <= s0 < t1:
+                    multiply(s0, n, (4,))
+                    nc.scalar.activation(
+                        y[:, s0 : s0 + n], acc[s0][:, 0:n], RELU, bias=b_sb[:, s0 // C : s0 // C + 1]
+                    )
+            for s0, n in groups[opened : opened + 2]:
+                multiply(s0, n, (0, 1, 2, 3))
+            opened += 2
+
+        def product(r, c0, c1):
+            p = keep.tile([P, c1 - c0], F32, name=f"p{r}_{c0}")
+            nc.vector.tensor_tensor(
+                p[:], y[:].indirect(pos_sb[r][:, c0 // 16 : c1 // 16]), gate_sb[:, r, c0:c1], MULT
+            )
+            return p
+
+        def add(x0, x1, name):
+            s = keep.tile([P, x0.shape[1]], F32, name=name)
+            nc.vector.tensor_tensor(s[:], x0[:], x1[:], ADD)
+            return s
+
+        pa = [product(r, 0, 512) for r in range(3)]
+        sa = add(pa[0], pa[1], "sa")
+        pa.append(product(3, 0, 512))
+        sa2 = add(sa, pa[2], "sa2")
+        pb = [product(0, 512, T)]
+        oa = add(sa2, pa[3], "oa")
+        nc.sync.dma_start(out[:, 0:512], oa[:])
+        pb += [product(r, 512, T) for r in (1, 2)]
+        sb = add(pb[0], pb[1], "sb")
+        pb.append(product(3, 512, T))
+        sb2 = add(sb, pb[2], "sb2")
+        ob = add(sb2, pb[3], "ob")
+        nc.sync.dma_start(out[:, 512:T], ob[:])

@@ -12,6 +12,7 @@ PASSES = K // K_PASS
 CHUNK = 512
 CHUNKS = S // CHUNK
 QUAD = 32
+HALF = S // 2
 LIVE = 4
 
 FLOPS = 2 * K * N * S
@@ -25,6 +26,7 @@ U8 = mybir.dt.uint8
 FP8X4 = mybir.dt.float8_e4m3fn_x4
 MULT = mybir.AluOpType.mult
 ADD = mybir.AluOpType.add
+MAX = mybir.AluOpType.max
 RELU = mybir.ActivationFunctionType.Relu
 
 
@@ -39,17 +41,19 @@ def tile_moe_tk_lin_relu_kernel(
 
         offs_sb = keep.tile([P, S // 16], U16, name="offs_sb")
         pos_sb = [keep.tile([P, T // 16], U16, name=f"pos_sb{r}") for r in range(TOP)]
-        codes = [keep.tile([P, T], U32, name=f"codes{a}", align_bytes=64) for a in range(PASSES)]
+        codes = [
+            keep.tile([P, T], U32, name=f"codes{a}", tag="late" if a == 2 else f"codes{a}", align_bytes=64)
+            for a in range(PASSES)
+        ]
         planes_a = keep.tile([P, T], U8, name="planes_a", align_bytes=64)
         planes_b = keep.tile([P, T], U8, name="planes_b", align_bytes=64)
         planes = keep.tile([P, T], U8, name="planes", tag="turns", align_bytes=64)
-        words = [keep.tile([P, S], U32, name=f"words{a}", align_bytes=64) for a in range(PASSES - 1)]
-        slot_planes = keep.tile([P, S], U8, name="slot_planes", align_bytes=64)
-        slot_plane4 = keep.tile([P, S], U8, name="slot_plane4", align_bytes=64)
+        words = [keep.tile([P, S], U32, name=f"words{a}", align_bytes=64) for a in range(PASSES - 2)]
+        slot_planes = [keep.tile([P, HALF], U8, name=f"slot_planes{h}", align_bytes=64) for h in range(2)]
+        slot_plane4 = [keep.tile([P, HALF], U8, name=f"slot_plane4{h}", align_bytes=64) for h in range(2)]
         w_sb = keep.tile([P, E * PASSES * N * PACK], U8, name="w_sb", align_bytes=64)
         ws_sb = keep.tile([P, E * PASSES * N], U8, name="ws_sb", align_bytes=64)
         b_sb = keep.tile([P, E], F32, name="b_sb")
-        gate_sb = keep.tile([P, TOP, T], F32, name="gate_sb")
         y = keep.tile([P, S], F32, name="y")
 
         warm = keep.tile([P, 1], F32, name="warm")
@@ -58,12 +62,16 @@ def tile_moe_tk_lin_relu_kernel(
 
         nc.gpsimd.memset(planes[:].bitcast(I32), 0)
         nc.gpsimd.memset(ws_sb[:].bitcast(I32), 0)
-        nc.gpsimd.memset(slot_plane4[:].bitcast(I32), 0)
+        for h in range(2):
+            nc.gpsimd.memset(slot_plane4[h][:].bitcast(I32), 0)
 
         raw, grouped = [], []
         for a in range(PASSES):
             raw.append(raws.tile([P, PACK, T], F32, name="raw"))
-            grouped.append(raws.tile([P, T * PACK], BF16, name="grouped", align_bytes=64))
+            if a < 4:
+                grouped.append(raws.tile([P, T * PACK], BF16, name="grouped", align_bytes=64))
+            else:
+                grouped.append(keep.tile([P, T * PACK], BF16, name="grouped4", tag="turns3", align_bytes=64))
 
         def load(a, c0, c1):
             nc.sync.dma_start(
@@ -107,7 +115,6 @@ def tile_moe_tk_lin_relu_kernel(
                 out=w_sb[:, e * half : (e + 2) * half].bitcast(I32).rearrange("p (g n) -> p g n", g=2 * PASSES),
                 in_=w_words[e : e + 2].rearrange("e a p n r -> p (e a) (n r)").bitcast(I32),
             )
-        nc.sync.dma_start(gate_sb[:], gate.rearrange("r n t -> n r t"))
         for tile, src in zip(pos_sb, (pos1, pos2, pos3, pos4)):
             nc.sync.dma_start(tile[:], src)
 
@@ -148,7 +155,8 @@ def tile_moe_tk_lin_relu_kernel(
                 acc[s0] = psum.tile([P, C], F32, name="acc")
             for a in passes:
                 g = s0 // C * PASSES + a
-                plane = slot_planes[4 * a : P, s0 : s0 + n] if a < 4 else slot_plane4[:, s0 : s0 + n]
+                h, h0 = s0 // HALF, s0 % HALF
+                plane = slot_planes[h][4 * a : P, h0 : h0 + n] if a < 4 else slot_plane4[h][:, h0 : h0 + n]
                 nc.tensor.matmul_mx(
                     out=acc[s0][:, 0:n],
                     lhsT=w_sb[:, g * 512 : (g + 1) * 512].bitcast(FP8X4),
@@ -159,18 +167,24 @@ def tile_moe_tk_lin_relu_kernel(
                     stop=(a == PASSES - 1),
                 )
 
-        for c in range(CHUNKS):
+        gate_sb = keep.tile([P, TOP, T], F32, name="gate_sb", tag="late", align_bytes=64)
+        nc.sync.dma_start(gate_sb[:], gate.rearrange("r n t -> n r t"))
+        words.append(keep.tile([P, S], U32, name="words3", tag="turns3", align_bytes=64))
+        for c in range(3):
             gather_words(3, c * CHUNK, (c + 1) * CHUNK)
-        for c in range(CHUNKS):
-            s0, s1 = c * CHUNK, (c + 1) * CHUNK
-            nc.vector.tensor_copy(slot_planes[:, s0:s1], planes[:].indirect(offs_sb[:, s0 // 16 : s1 // 16]))
-            if c in (2, 5):
-                h0 = s1 - 3 * CHUNK
-                for q in range(4):
-                    nc.sync.dma_start(
-                        out=slot_plane4[QUAD * q : QUAD * q + LIVE, h0:s1].bitcast(I32),
-                        in_=slot_planes[QUAD * q + 16 : QUAD * q + 20, h0:s1].bitcast(I32),
-                    )
+        for h in range(2):
+            for h0 in range(0, HALF, CHUNK):
+                s0 = h * HALF + h0
+                nc.vector.tensor_copy(
+                    slot_planes[h][:, h0 : h0 + CHUNK], planes[:].indirect(offs_sb[:, s0 // 16 : (s0 + CHUNK) // 16])
+                )
+            for q in range(4):
+                nc.sync.dma_start(
+                    out=slot_plane4[h][QUAD * q : QUAD * q + LIVE, :].bitcast(I32),
+                    in_=slot_planes[h][QUAD * q + 16 : QUAD * q + 20, :].bitcast(I32),
+                )
+        for c in range(3, CHUNKS):
+            gather_words(3, c * CHUNK, (c + 1) * CHUNK)
         words.append(keep.tile([P, S], U32, name="words4", tag="turns", align_bytes=64))
         groups = [(e * C, C) for e in range(E - 1)] + [(S - 256, 128), (S - 128, 128)]
         for s0, n in groups[:8]:
@@ -182,15 +196,17 @@ def tile_moe_tk_lin_relu_kernel(
             for s0, n in groups:
                 if t0 <= s0 < t1:
                     multiply(s0, n, (4,))
-                    nc.scalar.activation(
-                        y[:, s0 : s0 + n], acc[s0][:, 0:n], RELU, bias=b_sb[:, s0 // C : s0 // C + 1]
-                    )
+                    bias = b_sb[:, s0 // C : s0 // C + 1]
+                    if t1 == S:
+                        nc.vector.tensor_scalar(y[:, s0 : s0 + n], acc[s0][:, 0:n], bias, 0.0, ADD, MAX)
+                    else:
+                        nc.scalar.activation(y[:, s0 : s0 + n], acc[s0][:, 0:n], RELU, bias=bias)
             for s0, n in groups[opened : opened + 2]:
                 multiply(s0, n, (0, 1, 2, 3))
             opened += 2
 
         def product(r, c0, c1):
-            p = keep.tile([P, c1 - c0], F32, name=f"p{r}_{c0}")
+            p = keep.tile([P, c1 - c0], F32, name=f"p{r}_{c0}", tag=f"p{r}")
             nc.vector.tensor_tensor(
                 p[:], y[:].indirect(pos_sb[r][:, c0 // 16 : c1 // 16]), gate_sb[:, r, c0:c1], MULT
             )

@@ -13,6 +13,7 @@ CHUNK = 512
 CHUNKS = S // CHUNK
 QUAD = 32
 HALF = S // 2
+SPLIT = 2560
 LIVE = 4
 
 FLOPS = 2 * K * N * S
@@ -60,7 +61,7 @@ def tile_moe_tk_lin_relu_kernel(
         nc.vector.memset(warm[:], 0.0)
         nc.scalar.activation(warm[:], warm[:], RELU)
 
-        nc.gpsimd.memset(planes[:].bitcast(I32), 0)
+        nc.gpsimd.memset(planes_a[:].bitcast(I32), 0)
         nc.gpsimd.memset(ws_sb[:].bitcast(I32), 0)
         for h in range(2):
             nc.gpsimd.memset(slot_plane4[h][:].bitcast(I32), 0)
@@ -94,14 +95,22 @@ def tile_moe_tk_lin_relu_kernel(
             )
 
         def gather_words(a, s0, s1):
-            nc.vector.tensor_copy(words[a][:, s0:s1], codes[a][:].indirect(offs_sb[:, s0 // 16 : s1 // 16]))
+            nc.vector.tensor_copy(words_of(a, s0, s1 - s0), codes[a][:].indirect(offs_sb[:, s0 // 16 : s1 // 16]))
+
+        def words_of(a, s0, n):
+            if a == 4:
+                return words[4][:, S - SPLIT + s0 : S - SPLIT + s0 + n]
+            if a == 3 and s0 >= SPLIT:
+                return words[4][:, s0 - SPLIT : s0 - SPLIT + n]
+            return words[a][:, s0 : s0 + n]
 
         for c0 in range(0, T, 256):
             load(0, c0, c0 + 256)
         nc.sync.dma_start(offs_sb[:], offs)
-        for a in range(1, PASSES):
-            load(a, 0, 512)
-            load(a, 512, T)
+        load(1, 0, 512)
+        load(1, 512, T)
+        for a in range(2, PASSES):
+            load(a, 0, T)
         ws_rows = w_scales.rearrange("e a q n -> q (e a) n").bitcast(I32)
         for q in range(4):
             nc.sync.dma_start(
@@ -129,19 +138,15 @@ def tile_moe_tk_lin_relu_kernel(
 
         for a in range(3):
             for c in range(CHUNKS):
-                gather_words(a, c * CHUNK, (c + 1) * CHUNK)
-                if c == 2:
+                if c == 4:
                     quantise(a + 1, 0, 512)
-                if c == 3:
+                if c == 5:
                     quantise(a + 1, 512, T)
-                if a == 2 and c == 4:
-                    quantise(4, 0, 512)
-                    quantise(4, 512, T)
-        for q in range(4):
-            nc.scalar.dma_start(
-                out=planes[QUAD * q : QUAD * q + 16, :].bitcast(I32),
-                in_=planes_a[QUAD * q : QUAD * q + 16, :].bitcast(I32),
-            )
+                    if a == 2:
+                        nc.scalar.dma_start(out=planes[:].bitcast(I32), in_=planes_a[:].bitcast(I32))
+                        quantise(4, 0, 512)
+                        quantise(4, 512, T)
+                gather_words(a, c * CHUNK, (c + 1) * CHUNK)
         for q in range(4):
             nc.scalar.dma_start(
                 out=planes[QUAD * q + 16 : QUAD * q + 20, :].bitcast(I32),
@@ -161,7 +166,7 @@ def tile_moe_tk_lin_relu_kernel(
                     out=acc[s0][:, 0:n],
                     lhsT=w_sb[:, g * 512 : (g + 1) * 512].bitcast(FP8X4),
                     lhsT_scale=ws_sb[:, g * N : (g + 1) * N],
-                    rhs=words[a][:, s0 : s0 + n].bitcast(FP8X4),
+                    rhs=words_of(a, s0, n).bitcast(FP8X4),
                     rhs_scale=plane,
                     start=(a == 0),
                     stop=(a == PASSES - 1),
@@ -169,8 +174,8 @@ def tile_moe_tk_lin_relu_kernel(
 
         gate_sb = keep.tile([P, TOP, T], F32, name="gate_sb", tag="late", align_bytes=64)
         nc.sync.dma_start(gate_sb[:], gate.rearrange("r n t -> n r t"))
-        words.append(keep.tile([P, S], U32, name="words3", tag="turns3", align_bytes=64))
-        for c in range(3):
+        words.append(keep.tile([P, SPLIT], U32, name="words3", tag="turns3", align_bytes=64))
+        for c in range(5):
             gather_words(3, c * CHUNK, (c + 1) * CHUNK)
         for h in range(2):
             for h0 in range(0, HALF, CHUNK):
@@ -183,9 +188,9 @@ def tile_moe_tk_lin_relu_kernel(
                     out=slot_plane4[h][QUAD * q : QUAD * q + LIVE, :].bitcast(I32),
                     in_=slot_planes[h][QUAD * q + 16 : QUAD * q + 20, :].bitcast(I32),
                 )
-        for c in range(3, CHUNKS):
+        words.append(keep.tile([P, S - SPLIT + S], U32, name="words4", tag="turns", align_bytes=64))
+        for c in range(5, CHUNKS):
             gather_words(3, c * CHUNK, (c + 1) * CHUNK)
-        words.append(keep.tile([P, S], U32, name="words4", tag="turns", align_bytes=64))
         groups = [(e * C, C) for e in range(E - 1)] + [(S - 256, 128), (S - 128, 128)]
         for s0, n in groups[:8]:
             multiply(s0, n, (0, 1, 2, 3))

@@ -13,7 +13,7 @@ CHUNK = 512
 CHUNKS = S // CHUNK
 QUAD = 32
 HALF = S // 2
-SPLIT = 2560
+SPLIT = 2048
 LIVE = 4
 
 FLOPS = 2 * K * N * S
@@ -43,11 +43,11 @@ def tile_moe_tk_lin_relu_kernel(
         offs_sb = keep.tile([P, S // 16], U16, name="offs_sb")
         pos_sb = [keep.tile([P, T // 16], U16, name=f"pos_sb{r}") for r in range(TOP)]
         codes = [
-            keep.tile([P, T], U32, name=f"codes{a}", tag="late" if a == 2 else f"codes{a}", align_bytes=64)
+            keep.tile([P, T], U32, name=f"codes{a}", align_bytes=64)
             for a in range(PASSES)
         ]
         planes_a = keep.tile([P, T], U8, name="planes_a", align_bytes=64)
-        planes_b = keep.tile([P, T], U8, name="planes_b", align_bytes=64)
+        planes_b = keep.tile([P, T], U8, name="planes_b", tag="late", align_bytes=64)
         planes = keep.tile([P, T], U8, name="planes", tag="turns", align_bytes=64)
         words = [keep.tile([P, S], U32, name=f"words{a}", align_bytes=64) for a in range(PASSES - 2)]
         slot_planes = [keep.tile([P, HALF], U8, name=f"slot_planes{h}", align_bytes=64) for h in range(2)]
@@ -175,7 +175,7 @@ def tile_moe_tk_lin_relu_kernel(
         gate_sb = keep.tile([P, TOP, T], F32, name="gate_sb", tag="late", align_bytes=64)
         nc.sync.dma_start(gate_sb[:], gate.rearrange("r n t -> n r t"))
         words.append(keep.tile([P, SPLIT], U32, name="words3", tag="turns3", align_bytes=64))
-        for c in range(5):
+        for c in range(4):
             gather_words(3, c * CHUNK, (c + 1) * CHUNK)
         for h in range(2):
             for h0 in range(0, HALF, CHUNK):
@@ -189,49 +189,57 @@ def tile_moe_tk_lin_relu_kernel(
                     in_=slot_planes[h][QUAD * q + 16 : QUAD * q + 20, :].bitcast(I32),
                 )
         words.append(keep.tile([P, S - SPLIT + S], U32, name="words4", tag="turns", align_bytes=64))
-        for c in range(5, CHUNKS):
-            gather_words(3, c * CHUNK, (c + 1) * CHUNK)
         groups = [(e * C, C) for e in range(E - 1)] + [(S - 256, 128), (S - 128, 128)]
         for s0, n in groups[:8]:
             multiply(s0, n, (0, 1, 2, 3))
         opened = 8
-        edges = [0, 512, 1024, 1536, 2048, 2560, 2944, 3072]
+        edges = [0, 512, 1024, 1536, 2048, 2304, 2560, 2816, 2944, 3072]
         for t0, t1 in zip(edges, edges[1:]):
             gather_words(4, t0, t1)
+            if t1 == 1024:
+                gather_words(3, SPLIT, SPLIT + CHUNK)
+                gather_words(3, SPLIT + CHUNK, S)
             for s0, n in groups:
                 if t0 <= s0 < t1:
                     multiply(s0, n, (4,))
                     bias = b_sb[:, s0 // C : s0 // C + 1]
-                    if t1 == S:
+                    if s0 >= S - 2 * C:
                         nc.vector.tensor_scalar(y[:, s0 : s0 + n], acc[s0][:, 0:n], bias, 0.0, ADD, MAX)
                     else:
                         nc.scalar.activation(y[:, s0 : s0 + n], acc[s0][:, 0:n], RELU, bias=bias)
-            for s0, n in groups[opened : opened + 2]:
-                multiply(s0, n, (0, 1, 2, 3))
-            opened += 2
+            if t1 >= 1024:
+                for s0, n in groups[opened : opened + 2]:
+                    multiply(s0, n, (0, 1, 2, 3))
+                opened += 2
 
-        def product(r, c0, c1):
-            p = keep.tile([P, c1 - c0], F32, name=f"p{r}_{c0}", tag=f"p{r}")
+        spans = ((0, 640), (640, T))
+        terms = [[keep.tile([P, c1 - c0], F32, name=f"term{r}_{c0}") for r in range(TOP)] for c0, c1 in spans]
+        sums = [[keep.tile([P, c1 - c0], F32, name=f"sum{r}_{c0}") for r in range(TOP - 1)] for c0, c1 in spans]
+
+        def product(i, r):
+            c0, c1 = spans[i]
             nc.vector.tensor_tensor(
-                p[:], y[:].indirect(pos_sb[r][:, c0 // 16 : c1 // 16]), gate_sb[:, r, c0:c1], MULT
+                terms[i][r][:], y[:].indirect(pos_sb[r][:, c0 // 16 : c1 // 16]), gate_sb[:, r, c0:c1], MULT
             )
-            return p
 
-        def add(x0, x1, name):
-            s = keep.tile([P, x0.shape[1]], F32, name=name)
-            nc.vector.tensor_tensor(s[:], x0[:], x1[:], ADD)
-            return s
+        def add(i, r):
+            first = terms[i][0] if r == 0 else sums[i][r - 1]
+            nc.vector.tensor_tensor(sums[i][r][:], first[:], terms[i][r + 1][:], ADD)
+            if r == TOP - 2:
+                c0, c1 = spans[i]
+                nc.sync.dma_start(out[:, c0:c1], sums[i][r][:])
 
-        pa = [product(r, 0, 512) for r in range(3)]
-        sa = add(pa[0], pa[1], "sa")
-        pa.append(product(3, 0, 512))
-        sa2 = add(sa, pa[2], "sa2")
-        pb = [product(0, 512, T)]
-        oa = add(sa2, pa[3], "oa")
-        nc.sync.dma_start(out[:, 0:512], oa[:])
-        pb += [product(r, 512, T) for r in (1, 2)]
-        sb = add(pb[0], pb[1], "sb")
-        pb.append(product(3, 512, T))
-        sb2 = add(sb, pb[2], "sb2")
-        ob = add(sb2, pb[3], "ob")
-        nc.sync.dma_start(out[:, 512:T], ob[:])
+        product(0, 0)
+        product(0, 1)
+        product(0, 2)
+        add(0, 0)
+        product(0, 3)
+        add(0, 1)
+        product(1, 0)
+        add(0, 2)
+        product(1, 1)
+        product(1, 2)
+        add(1, 0)
+        product(1, 3)
+        add(1, 1)
+        add(1, 2)

@@ -86,7 +86,9 @@ def tile_moe_tk_lin_relu_kernel(
             if engine == "v":
                 nc.vector.tensor_copy(dst, src)
             else:
-                nc.scalar.copy(dst, src)
+                nc.scalar.copy(
+                    dst.rearrange("p (c i) j -> p c j i", i=4), raw[a][:, :, c0:c1].rearrange("p j (c i) -> p c j i", i=4)
+                )
 
         def quantise(a, c0, c1):
             plane = planes_a[4 * a : P, c0:c1] if a < 4 else planes_b[:, c0:c1]

from contextlib import ExitStack

import concourse.mybir as mybir

K, T, E, C, N = 2560, 768, 12, 256, 128
TOP = 4
S = E * C
P = 128
PACK = 4
K_PASS = P * PACK
PASSES = K // K_PASS
CHUNK = 512
CHUNKS = S // CHUNK
QUAD = 32
HALF = S // 2
SPLIT = 2048
LIVE = 4

FLOPS = 2 * K * N * S

F32 = mybir.dt.float32
BF16 = mybir.dt.bfloat16
U32 = mybir.dt.uint32
I32 = mybir.dt.int32
U16 = mybir.dt.uint16
U8 = mybir.dt.uint8
FP8X4 = mybir.dt.float8_e4m3fn_x4
MULT = mybir.AluOpType.mult
ADD = mybir.AluOpType.add
MAX = mybir.AluOpType.max
RELU = mybir.ActivationFunctionType.Relu


def tile_moe_tk_lin_relu_kernel(
    tc, xT, w_words, w_scales, b, gate, offs, pos1, pos2, pos3, pos4, out
):
    nc = tc.nc
    with ExitStack() as ctx:
        keep = ctx.enter_context(tc.tile_pool(name="keep", bufs=1))
        raws = ctx.enter_context(tc.tile_pool(name="raws", bufs=3))
        psum = ctx.enter_context(tc.psum_pool(name="psum", bufs=8))

        offs_sb = keep.tile([P, S // 16], U16, name="offs_sb")
        pos_sb = [keep.tile([P, T // 16], U16, name=f"pos_sb{r}") for r in range(TOP)]
        codes = [
            keep.tile([P, T], U32, name=f"codes{a}", align_bytes=64)
            for a in range(PASSES)
        ]
        planes_a = keep.tile([P, T], U8, name="planes_a", align_bytes=64)
        planes_b = keep.tile([P, T], U8, name="planes_b", tag="late", align_bytes=64)
        planes = keep.tile([P, T], U8, name="planes", tag="turns", align_bytes=64)
        words = [keep.tile([P, S], U32, name=f"words{a}", align_bytes=64) for a in range(PASSES - 2)]
        slot_planes = [keep.tile([P, HALF], U8, name=f"slot_planes{h}", align_bytes=64) for h in range(2)]
        slot_plane4 = [keep.tile([P, HALF], U8, name=f"slot_plane4{h}", align_bytes=64) for h in range(2)]
        w_sb = keep.tile([P, E * PASSES * N * PACK], U8, name="w_sb", align_bytes=64)
        ws_sb = keep.tile([P, E * PASSES * N], U8, name="ws_sb", align_bytes=64)
        b_sb = keep.tile([P, E], F32, name="b_sb")
        y = keep.tile([P, S], F32, name="y")

        warm = keep.tile([P, 1], F32, name="warm")
        nc.vector.memset(warm[:], 0.0)
        nc.scalar.activation(warm[:], warm[:], RELU)

        nc.gpsimd.memset(planes_a[:].bitcast(I32), 0)
        nc.gpsimd.memset(ws_sb[:].bitcast(I32), 0)
        for h in range(2):
            nc.gpsimd.memset(slot_plane4[h][:].bitcast(I32), 0)

        raw, grouped = [], []
        for a in range(PASSES):
            raw.append(raws.tile([P, PACK, T], F32, name="raw"))
            if a < 4:
                grouped.append(raws.tile([P, T * PACK], BF16, name="grouped", align_bytes=64))
            else:
                grouped.append(keep.tile([P, T * PACK], BF16, name="grouped4", tag="turns3", align_bytes=64))

        def load(a, c0, c1):
            nc.sync.dma_start(
                out=raw[a][:, :, c0:c1],
                in_=xT[a * K_PASS : (a + 1) * K_PASS, c0:c1].rearrange("(p j) w -> p j w", j=PACK),
            )

        def interleave(engine, a, c0, c1):
            dst = grouped[a][:].rearrange("p (w j) -> p w j", j=PACK)[:, c0:c1, :]
            src = raw[a][:, :, c0:c1].rearrange("p j w -> p w j")
            if engine == "v":
                nc.vector.tensor_copy(dst, src)
            else:
                nc.scalar.copy(
                    dst.rearrange("p (c i) j -> p c j i", i=4), raw[a][:, :, c0:c1].rearrange("p j (c i) -> p c j i", i=4)
                )

        def quantise(a, c0, c1):
            plane = planes_a[4 * a : P, c0:c1] if a < 4 else planes_b[:, c0:c1]
            nc.vector.quantize_mx(
                out=codes[a][:, c0:c1].bitcast(FP8X4), scales=plane, in_=grouped[a][:, c0 * PACK : c1 * PACK]
            )

        def gather_words(a, s0, s1):
            nc.vector.tensor_copy(words_of(a, s0, s1 - s0), codes[a][:].indirect(offs_sb[:, s0 // 16 : s1 // 16]))

        def words_of(a, s0, n):
            if a == 4:
                return words[4][:, S - SPLIT + s0 : S - SPLIT + s0 + n]
            if a == 3 and s0 >= SPLIT:
                return words[4][:, s0 - SPLIT : s0 - SPLIT + n]
            return words[a][:, s0 : s0 + n]

        for c0 in range(0, T, 256):
            load(0, c0, c0 + 256)
        nc.sync.dma_start(offs_sb[:], offs)
        load(1, 0, 512)
        load(1, 512, T)
        for a in range(2, PASSES):
            load(a, 0, T)
        ws_rows = w_scales.rearrange("e a q n -> q (e a) n").bitcast(I32)
        for q in range(4):
            nc.sync.dma_start(
                out=ws_sb[QUAD * q : QUAD * q + LIVE, :].bitcast(I32).rearrange("p (g n) -> p g n", g=E * PASSES),
                in_=ws_rows[LIVE * q : LIVE * (q + 1)],
            )
        nc.sync.dma_start(b_sb[:], b)
        half = PASSES * N * PACK
        for e in range(0, E, 2):
            nc.sync.dma_start(
                out=w_sb[:, e * half : (e + 2) * half].bitcast(I32).rearrange("p (g n) -> p g n", g=2 * PASSES),
                in_=w_words[e : e + 2].rearrange("e a p n r -> p (e a) (n r)").bitcast(I32),
            )
        for tile, src in zip(pos_sb, (pos1, pos2, pos3, pos4)):
            nc.sync.dma_start(tile[:], src)

        for c0 in range(0, T, 256):
            interleave("v", 0, c0, c0 + 128)
            interleave("s", 0, c0 + 128, c0 + 256)
            quantise(0, c0, c0 + 128)
            quantise(0, c0 + 128, c0 + 256)
        for a in range(1, PASSES):
            interleave("s", a, 0, 512)
            interleave("s", a, 512, T)

        for a in range(3):
            for c in range(CHUNKS):
                if c == 4:
                    quantise(a + 1, 0, 512)
                if c == 5:
                    quantise(a + 1, 512, T)
                    if a == 2:
                        nc.scalar.dma_start(out=planes[:].bitcast(I32), in_=planes_a[:].bitcast(I32))
                        quantise(4, 0, 512)
                        quantise(4, 512, T)
                gather_words(a, c * CHUNK, (c + 1) * CHUNK)
        for q in range(4):
            nc.scalar.dma_start(
                out=planes[QUAD * q + 16 : QUAD * q + 20, :].bitcast(I32),
                in_=planes_b[QUAD * q : QUAD * q + LIVE, :].bitcast(I32),
            )

        acc = {}

        def multiply(s0, n, passes):
            if s0 not in acc:
                acc[s0] = psum.tile([P, C], F32, name="acc")
            for a in passes:
                g = s0 // C * PASSES + a
                h, h0 = s0 // HALF, s0 % HALF
                plane = slot_planes[h][4 * a : P, h0 : h0 + n] if a < 4 else slot_plane4[h][:, h0 : h0 + n]
                nc.tensor.matmul_mx(
                    out=acc[s0][:, 0:n],
                    lhsT=w_sb[:, g * 512 : (g + 1) * 512].bitcast(FP8X4),
                    lhsT_scale=ws_sb[:, g * N : (g + 1) * N],
                    rhs=words_of(a, s0, n).bitcast(FP8X4),
                    rhs_scale=plane,
                    start=(a == 0),
                    stop=(a == PASSES - 1),
                )

        gate_sb = keep.tile([P, TOP, T], F32, name="gate_sb", tag="late", align_bytes=64)
        nc.sync.dma_start(gate_sb[:], gate.rearrange("r n t -> n r t"))
        words.append(keep.tile([P, SPLIT], U32, name="words3", tag="turns3", align_bytes=64))
        for c in range(4):
            gather_words(3, c * CHUNK, (c + 1) * CHUNK)
        for h in range(2):
            for h0 in range(0, HALF, CHUNK):
                s0 = h * HALF + h0
                nc.vector.tensor_copy(
                    slot_planes[h][:, h0 : h0 + CHUNK], planes[:].indirect(offs_sb[:, s0 // 16 : (s0 + CHUNK) // 16])
                )
            for q in range(4):
                nc.sync.dma_start(
                    out=slot_plane4[h][QUAD * q : QUAD * q + LIVE, :].bitcast(I32),
                    in_=slot_planes[h][QUAD * q + 16 : QUAD * q + 20, :].bitcast(I32),
                )
        words.append(keep.tile([P, S - SPLIT + S], U32, name="words4", tag="turns", align_bytes=64))
        groups = [(e * C, C) for e in range(E - 1)] + [(S - 256, 128), (S - 128, 128)]
        for s0, n in groups[:8]:
            multiply(s0, n, (0, 1, 2, 3))
        opened = 8
        edges = [0, 512, 1024, 1536, 2048, 2304, 2560, 2816, 2944, 3072]
        for t0, t1 in zip(edges, edges[1:]):
            gather_words(4, t0, t1)
            if t1 == 1024:
                gather_words(3, SPLIT, SPLIT + CHUNK)
                gather_words(3, SPLIT + CHUNK, S)
            for s0, n in groups:
                if t0 <= s0 < t1:
                    multiply(s0, n, (4,))
                    bias = b_sb[:, s0 // C : s0 // C + 1]
                    if s0 >= S - 2 * C:
                        nc.vector.tensor_scalar(y[:, s0 : s0 + n], acc[s0][:, 0:n], bias, 0.0, ADD, MAX)
                    else:
                        nc.scalar.activation(y[:, s0 : s0 + n], acc[s0][:, 0:n], RELU, bias=bias)
            if t1 >= 1024:
                for s0, n in groups[opened : opened + 2]:
                    multiply(s0, n, (0, 1, 2, 3))
                opened += 2

        spans = ((0, 640), (640, T))
        terms = [[keep.tile([P, c1 - c0], F32, name=f"term{r}_{c0}") for r in range(TOP)] for c0, c1 in spans]
        sums = [[keep.tile([P, c1 - c0], F32, name=f"sum{r}_{c0}") for r in range(TOP - 1)] for c0, c1 in spans]

        def product(i, r):
            c0, c1 = spans[i]
            nc.vector.tensor_tensor(
                terms[i][r][:], y[:].indirect(pos_sb[r][:, c0 // 16 : c1 // 16]), gate_sb[:, r, c0:c1], MULT
            )

        def add(i, r):
            first = terms[i][0] if r == 0 else sums[i][r - 1]
            nc.vector.tensor_tensor(sums[i][r][:], first[:], terms[i][r + 1][:], ADD)
            if r == TOP - 2:
                c0, c1 = spans[i]
                nc.sync.dma_start(out[:, c0:c1], sums[i][r][:])

        product(0, 0)
        product(0, 1)
        product(0, 2)
        add(0, 0)
        product(0, 3)
        add(0, 1)
        product(1, 0)
        add(0, 2)
        product(1, 1)
        product(1, 2)
        add(1, 0)
        product(1, 3)
        add(1, 1)
        add(1, 2)
